import numpy as np, ml_dtypes
CORES = [4,12,20,28,44,60,76,84,92,108,116,124]
N = 12
TK = 64
def gelu(z): return 0.5 * z * (1.0 + np.tanh(0.7978845608028654 * (z + 0.044715 * z ** 3)))
def setup_inputs(rng):
    return {"x": rng.standard_normal((N, 128, TK), dtype=np.float32).astype(ml_dtypes.bfloat16), "w1": (rng.standard_normal((N, 128, 128), dtype=np.float32) / 8).astype(ml_dtypes.bfloat16), "w2": (rng.standard_normal((N, 128, 128), dtype=np.float32) / 8).astype(ml_dtypes.bfloat16)}
def setup_inputs_big(rng):
    d = setup_inputs(rng)
    for k in ("x",): d[k] = (d[k].astype(np.float32) * 1024.0).astype(d[k].dtype)
    return d
def setup_inputs_small(rng):
    d = setup_inputs(rng)
    for k in ("x",): d[k] = (d[k].astype(np.float32) * (1 / 1024.0)).astype(d[k].dtype)
    return d
def setup_inputs_apart(rng):
    d = setup_inputs(rng)
    f = (10.0 ** rng.permutation(np.linspace(-1.5, 1.5, N))).astype(np.float32).reshape(N, 1, 1)
    for k in ("x",): d[k] = (d[k].astype(np.float32) * f).astype(d[k].dtype)
    return d
def reference(x, w1, w2):
    X, W1, W2 = x.astype(np.float64), w1.astype(np.float64), w2.astype(np.float64)
    y = np.zeros((N, 128, TK))
    for r in range(N):
        for j in range(N):
            y[r] += W2[j].T @ (gelu(W1[j].T @ X[r]))
    return {"y": y.astype(ml_dtypes.bfloat16)}

@@ -1,0 +1,206 @@
+from concourse.bass import DstId, RemoteDMATransfer
+from concourse.mybir import AluOpType, ActivationFunctionType
+
+TK = 64
+GS = 4
+NJ = 3
+
+SCRATCH = {
+    "xsrc": ("dram", [128, TK], "bfloat16"),
+    "wst": ("sbuf", [128, 256], "bfloat16"),
+    "pl": ("sbuf", [128, NJ * TK], "bfloat16"),
+    "acc": ("sbuf", [128, TK], "float32"),
+    "yout": ("sbuf", [128, TK], "bfloat16"),
+    "xd": ("dram", [2, 128, TK], "bfloat16"),
+    "xs": ("sbuf", [128, NJ * TK], "bfloat16"),
+    "wbuf": ("sbuf", [128, GS * 256], "bfloat16"),
+    "hs": ("sbuf", [128, GS * NJ * TK], "bfloat16"),
+    "ps": ("sbuf", [128, NJ * TK], "bfloat16"),
+}
+for _i in range(GS):
+    SCRATCH["hb%d" % _i] = ("psum", [128, 512], "float32")
+for _j in range(NJ):
+    SCRATCH["yb%d" % _j] = ("psum", [128, 512], "float32")
+
+SEMAPHORES = ["ldx", "ldw", "snd", "sadd", "sy", "sst", "xown", "xpeer", "xe", "xl0", "xl1"]
+SEMAPHORES += ["p%d" % _j for _j in range(NJ)] + ["w%d" % _i for _i in range(GS)]
+SEMAPHORES += ["y2_%d" % _j for _j in range(NJ)] + ["cp%d" % _j for _j in range(NJ)]
+SEMAPHORES += ["m1_%d_%d" % (_j, _i) for _j in range(NJ) for _i in range(GS)]
+SEMAPHORES += ["ac_%d_%d" % (_j, _i) for _j in range(NJ) for _i in range(GS)]
+
+
+def _plan(T, topo):
+    ch = topo.chip
+    ranks = list(T.cores)
+    a = [r for r in ranks if ch(r) == ch(ranks[0]) or topo.same_plane(ch(r), ch(ranks[0]))]
+    b = [r for r in ranks if r not in a]
+    minor, major = (a, b) if len(a) < len(b) else (b, a)
+    g1 = [o for e in minor for o in major if topo.mates(ch(e), ch(o))]
+    g2 = [o for o in major if o not in g1]
+    groups = [minor, g1, g2]
+    every = range(topo.CHIPS * topo.CORES_PER_CHIP)
+    site, relay = {}, {}
+    for gi, grp in enumerate(groups):
+        far = groups[1][0] if gi == 0 else groups[0][0]
+        for r in grp:
+            ports = [c for c in every if c != r and ch(c) == ch(r) and topo.die(c) == topo.die(r)
+                     and topo.may_write(c, far)]
+            site[r] = ports[0]
+            if gi == 0:
+                relay[r] = ports[1]
+    return groups, site, relay
+
+
+def _engines(topo, core):
+    every = range(topo.CHIPS * topo.CORES_PER_CHIP)
+    near = [c for c in every if c != core and topo.chip(c) == topo.chip(core)][0]
+    far = [c for c in every if topo.chip(c) != topo.chip(core)][0]
+    on, off = topo.mask(core, near), topo.mask(core, far)
+    lo = [e for e in range(on.bit_length()) if (off >> e) & 1]
+    hi = [e for e in range(on.bit_length()) if (on >> e) & 1 and not (off >> e) & 1]
+    return lo, hi
+
+
+def _mask(engs):
+    m = 0
+    for e in engs:
+        m |= 1 << e
+    return m
+
+
+def _tr(topo, src, dsts, cores, engs, sem):
+    ids = []
+    for c in cores:
+        rid, pid, _ = topo.addr(c)
+        ids.append(DstId(rid=rid, pnc=pid))
+    return RemoteDMATransfer(dst_ids=ids, dma_engine_mask=_mask(engs), remote_sem=sem, srcs=[src], dsts=list(dsts))
+
+
+def _cols(j):
+    return slice(j * TK, (j + 1) * TK)
+
+
+def _xslots(gi):
+    return [[0, 1, 2], [1, 2, 0], [2, 1, 0]][gi]
+
+
+def rank_program(g, core, T, topo):
+    groups, site, relay = _plan(T, topo)
+    S = T.sem
+    lo, hi = _engines(topo, core)
+    where = {r: (gi, k) for gi, grp in enumerate(groups) for k, r in enumerate(grp)}
+    NX = 2
+    NWON = 4
+    NE = len(lo)
+
+    if core in where:
+        gi, k = where[core]
+        g.sync.dma_start(T.xsrc[:, :], T.x[:, :]).then_inc(S.ldx, 16)
+        g.scalar.dma_start(T.wst[:, 0:128], T.w1[:, :]).then_inc(S.ldw, 16)
+        g.sync.dma_start(T.wst[:, 128:256], T.w2[:, :]).then_inc(S.ldw, 16)
+        g.wait_ge(S.ldx, 16)
+        if gi == 0:
+            second = _tr(topo, T.xsrc[:, :], [T.xd[0]], [relay[core]], lo[NX:2 * NX], S.xown)
+        else:
+            second = _tr(topo, T.xsrc[:, :], [T.xd[1]], [site[groups[3 - gi][k]]], lo[NX:2 * NX], S.xpeer)
+        g.remote_dma_fused([_tr(topo, T.xsrc[:, :], [T.xd[0]], [site[core]], lo[0:NX], S.xown), second],
+                           local_sem=S.snd)
+        g.wait_ge(S.ldw, 32)
+        others = [site[groups[gi][(k + d) % GS]] for d in range(1, GS)]
+        slot = T.wbuf[:, k * 256:(k + 1) * 256]
+        g.remote_dma_fused([_tr(topo, T.wst[:, :], [slot] * len(others), others, lo, S["w%d" % k]),
+                            _tr(topo, T.wst[:, :], [slot], [site[core]], hi[0:NWON], S["w%d" % k])],
+                           local_sem=S.snd)
+        a, b, c = _xslots(gi)
+        v = g.vector
+        v.wait_ge(S["p%d" % a], NE)
+        v.wait_ge(S["p%d" % b], NE)
+        v.tensor_tensor(T.acc[:, :], T.pl[:, _cols(a)], T.pl[:, _cols(b)], AluOpType.add).then_inc(S.sadd, 1)
+        v.wait_ge(S["p%d" % c], NE)
+        v.wait_ge(S.sadd, 1)
+        v.tensor_tensor(T.yout[:, :], T.acc[:, :], T.pl[:, _cols(c)], AluOpType.add).then_inc(S.sy, 1)
+        g.sync.wait_ge(S.sy, 1)
+        g.sync.dma_start(T.y[:, :], T.yout[:, :]).then_inc(S.sst, 16)
+        g.sync.wait_ge(S.sst, 16)
+        g.wait_ge(S.snd, 2 * NX + NE + NWON)
+        return
+
+    for r, c in relay.items():
+        if c == core:
+            k = where[r][1]
+            g.wait_ge(S.xown, NX)
+            g.remote_dma_fused([_tr(topo, T.xd[0], [T.xs[:, _cols(2)]], [site[groups[2][k]]], lo, S.xl0)],
+                               local_sem=S.snd)
+            g.wait_ge(S.snd, NE)
+            return
+
+    owner = [r for r, c in site.items() if c == core]
+    if not owner:
+        return
+
+    r = owner[0]
+    gi, k = where[r]
+    slots = _xslots(gi)
+    te, sc, ve = g.tensor, g.scalar, g.vector
+
+    g.wait_ge(S.xown, NX)
+    if gi == 0:
+        fwd = _tr(topo, T.xd[0], [T.xs[:, _cols(2)]], [site[groups[1][k]]], lo, S.xl0)
+    else:
+        fwd = _tr(topo, T.xd[0], [T.xs[:, _cols(gi)]], [site[groups[0][k]]], lo, S["xl%d" % (gi - 1)])
+    g.remote_dma_fused([fwd], local_sem=S.snd)
+    sent = NE
+
+    g.sync.wait_ge(S.xown, NX)
+    g.sync.dma_start(T.xs[:, _cols(0)], T.xd[0]).then_inc(S.xe, 16)
+    early = 1
+    if gi != 0:
+        sc.wait_ge(S.xpeer, NX)
+        sc.dma_start(T.xs[:, _cols(1)], T.xd[1]).then_inc(S.xe, 16)
+        early = 2
+
+    jobs = [(0, early, [(S.xe, 16 * early)])]
+    for n, s in enumerate(range(early, NJ)):
+        jobs.append((s, 1, [(S["xl%d" % n], NE)]))
+    order = [(k - d) % GS for d in range(GS)]
+
+    for j, (s0, ns, waits) in enumerate(jobs):
+        c0, c1 = s0 * TK, (s0 + ns) * TK
+        for sem, val in waits:
+            te.wait_ge(sem, val)
+
+        def mm1(i):
+            m = order[i]
+            if j == 0:
+                te.wait_ge(S["w%d" % m], NWON if m == k else NE)
+            hb = T["hb%d" % i]
+            te.matmul(hb[:, c0:c1], T.wbuf[:, m * 256:m * 256 + 128], T.xs[:, c0:c1], True, True) \
+                .then_inc(S["m1_%d_%d" % (j, i)], 1)
+            sc.wait_ge(S["m1_%d_%d" % (j, i)], 1)
+            sc.activation(T.hs[:, i * NJ * TK + c0:i * NJ * TK + c1], hb[:, c0:c1],
+                          ActivationFunctionType.Gelu_apprx_tanh).then_inc(S["ac_%d_%d" % (j, i)], 1)
+
+        def mm2(i):
+            m = order[i]
+            te.wait_ge(S["ac_%d_%d" % (j, i)], 1)
+            te.matmul(T["yb%d" % j][:, 0:c1 - c0], T.wbuf[:, m * 256 + 128:(m + 1) * 256],
+                      T.hs[:, i * NJ * TK + c0:i * NJ * TK + c1], i == 0, i == GS - 1) \
+                .then_inc(S["y2_%d" % j], 1)
+
+        mm1(0)
+        for i in range(1, GS):
+            mm1(i)
+            mm2(i - 1)
+        mm2(GS - 1)
+        ve.wait_ge(S["y2_%d" % j], GS)
+        ve.tensor_copy(T.ps[:, c0:c1], T["yb%d" % j][:, 0:c1 - c0]).then_inc(S["cp%d" % j], 1)
+
+        g.wait_ge(S["cp%d" % j], 1)
+        trs = []
+        for s in range(s0, s0 + ns):
+            dst = groups[slots[s]][k]
+            engs = hi if topo.chip(dst) == topo.chip(core) else lo
+            trs.append(_tr(topo, T.ps[:, _cols(s)], [T.pl[:, _cols(gi)]], [dst], engs[0:NE], S["p%d" % gi]))
+            sent += NE
+        g.remote_dma_fused(trs, local_sem=S.snd)
+    g.wait_ge(S.snd, sent)

@@ -4,29 +4,29 @@ from concourse.mybir import AluOpType, ActivationFunctionType
 TK = 64
 GS = 4
 NJ = 3
+NC = NJ * TK
+NST = 3
 
 SCRATCH = {
     "xsrc": ("dram", [128, TK], "bfloat16"),
     "wst": ("sbuf", [128, 256], "bfloat16"),
-    "pl": ("sbuf", [128, NJ * TK], "bfloat16"),
+    "pl": ("sbuf", [128, 2 * NC], "bfloat16"),
     "acc": ("sbuf", [128, TK], "float32"),
     "yout": ("sbuf", [128, TK], "bfloat16"),
     "xd": ("dram", [2, 128, TK], "bfloat16"),
-    "xs": ("sbuf", [128, NJ * TK], "bfloat16"),
+    "xs": ("sbuf", [128, NC], "bfloat16"),
     "wbuf": ("sbuf", [128, GS * 256], "bfloat16"),
-    "hs": ("sbuf", [128, GS * NJ * TK], "bfloat16"),
-    "ps": ("sbuf", [128, NJ * TK], "bfloat16"),
+    "hs": ("sbuf", [128, NST * NC], "bfloat16"),
+    "ps": ("sbuf", [128, NC], "bfloat16"),
 }
-for _i in range(GS):
+for _i in range(NST):
     SCRATCH["hb%d" % _i] = ("psum", [128, 512], "float32")
-for _j in range(NJ):
-    SCRATCH["yb%d" % _j] = ("psum", [128, 512], "float32")
+    SCRATCH["yb%d" % _i] = ("psum", [128, 512], "float32")
 
-SEMAPHORES = ["ldx", "ldw", "snd", "sadd", "sy", "sst", "xown", "xpeer", "xe", "xl0", "xl1"]
-SEMAPHORES += ["p%d" % _j for _j in range(NJ)] + ["w%d" % _i for _i in range(GS)]
-SEMAPHORES += ["y2_%d" % _j for _j in range(NJ)] + ["cp%d" % _j for _j in range(NJ)]
-SEMAPHORES += ["m1_%d_%d" % (_j, _i) for _j in range(NJ) for _i in range(GS)]
-SEMAPHORES += ["ac_%d_%d" % (_j, _i) for _j in range(NJ) for _i in range(GS)]
+SEMAPHORES = ["ldx", "ldw", "snd", "sadd", "sy", "sst", "xown", "xpeer", "xe", "xe1", "y2", "cp"]
+SEMAPHORES += ["xg%d" % _j for _j in range(NJ)] + ["p%d" % _j for _j in range(2 * NJ)]
+SEMAPHORES += ["w%d" % _i for _i in range(GS)] + ["v%d" % _i for _i in range(GS)]
+SEMAPHORES += ["m1_%d" % _i for _i in range(NST)] + ["ac_%d" % _i for _i in range(NST)]
 
 
 def _plan(T, topo):
@@ -39,16 +39,14 @@ def _plan(T, topo):
     g2 = [o for o in major if o not in g1]
     groups = [minor, g1, g2]
     every = range(topo.CHIPS * topo.CORES_PER_CHIP)
-    site, relay = {}, {}
+    sites, relay = ({}, {}), {}
     for gi, grp in enumerate(groups):
         far = groups[1][0] if gi == 0 else groups[0][0]
         for r in grp:
-            ports = [c for c in every if c != r and ch(c) == ch(r) and topo.die(c) == topo.die(r)
-                     and topo.may_write(c, far)]
-            site[r] = ports[0]
-            if gi == 0:
-                relay[r] = ports[1]
-    return groups, site, relay
+            ports = [c for c in every if c != r and ch(c) == ch(r) and topo.may_write(c, far)]
+            sites[0][r] = [c for c in ports if topo.die(c) == topo.die(r)][0]
+            sites[1][r], relay[r] = [c for c in ports if topo.die(c) != topo.die(r)][0:2]
+    return groups, sites, relay
 
 
 def _engines(topo, core):
@@ -85,13 +83,20 @@ def _xslots(gi):
 
 
 def rank_program(g, core, T, topo):
-    groups, site, relay = _plan(T, topo)
+    groups, sites, relay = _plan(T, topo)
+    A, B = sites
     S = T.sem
     lo, hi = _engines(topo, core)
     where = {r: (gi, k) for gi, grp in enumerate(groups) for k, r in enumerate(grp)}
-    NX = 2
-    NWON = 4
     NE = len(lo)
+    NH = NE // 2
+    NP = NH
+    NX = 2
+
+    def xfwd(k, gi, kind, to):
+        g.wait_ge(S.xown, NX)
+        g.remote_dma_fused([_tr(topo, T.xd[0], [T.xs[:, _cols(_xslots(gs).index(gi))] for gs in to],
+                                [sites[kind][groups[gs][k]] for gs in to], lo, S["xg%d" % gi])], local_sem=S.snd)
 
     if core in where:
         gi, k = where[core]
@@ -99,108 +104,130 @@ def rank_program(g, core, T, topo):
         g.scalar.dma_start(T.wst[:, 0:128], T.w1[:, :]).then_inc(S.ldw, 16)
         g.sync.dma_start(T.wst[:, 128:256], T.w2[:, :]).then_inc(S.ldw, 16)
         g.wait_ge(S.ldx, 16)
-        if gi == 0:
-            second = _tr(topo, T.xsrc[:, :], [T.xd[0]], [relay[core]], lo[NX:2 * NX], S.xown)
-        else:
-            second = _tr(topo, T.xsrc[:, :], [T.xd[1]], [site[groups[3 - gi][k]]], lo[NX:2 * NX], S.xpeer)
-        g.remote_dma_fused([_tr(topo, T.xsrc[:, :], [T.xd[0]], [site[core]], lo[0:NX], S.xown), second],
-                           local_sem=S.snd)
+        trs = [_tr(topo, T.xsrc[:, :], [T.xd[0], T.xd[0]], [B[core], relay[core]], hi[0:NX], S.xown),
+               _tr(topo, T.xsrc[:, :], [T.xd[0]], [A[core]], hi[NX:2 * NX], S.xown)]
+        sent = 2 * NX
+        if gi != 0:
+            trs.append(_tr(topo, T.xsrc[:, :], [T.xd[1]], [A[groups[3 - gi][k]]], lo[0:NH], S.xpeer))
+            sent += NH
+        g.remote_dma_fused(trs, local_sem=S.snd)
         g.wait_ge(S.ldw, 32)
-        others = [site[groups[gi][(k + d) % GS]] for d in range(1, GS)]
         slot = T.wbuf[:, k * 256:(k + 1) * 256]
-        g.remote_dma_fused([_tr(topo, T.wst[:, :], [slot] * len(others), others, lo, S["w%d" % k]),
-                            _tr(topo, T.wst[:, :], [slot], [site[core]], hi[0:NWON], S["w%d" % k])],
+        nb = [A[groups[gi][(k + 1) % GS]], A[groups[gi][(k - 1) % GS]]]
+        g.remote_dma_fused([_tr(topo, T.wst[:, :], [slot, slot], [B[core], A[core]], hi, S["w%d" % k]),
+                            _tr(topo, T.wst[:, :], [slot, slot], nb, lo, S["w%d" % k])],
                            local_sem=S.snd)
-        a, b, c = _xslots(gi)
+        g.remote_dma_fused([_tr(topo, T.wst[:, 0:128], [T.wbuf[:, k * 256:k * 256 + 128]],
+                                [B[groups[gi][(k + 2) % GS]]], lo, S["v%d" % k])], local_sem=S.snd)
+        sent += 3 * NE
+        order = [2 * gs + t for gs in _xslots(gi) for t in range(2)]
         v = g.vector
-        v.wait_ge(S["p%d" % a], NE)
-        v.wait_ge(S["p%d" % b], NE)
-        v.tensor_tensor(T.acc[:, :], T.pl[:, _cols(a)], T.pl[:, _cols(b)], AluOpType.add).then_inc(S.sadd, 1)
-        v.wait_ge(S["p%d" % c], NE)
-        v.wait_ge(S.sadd, 1)
-        v.tensor_tensor(T.yout[:, :], T.acc[:, :], T.pl[:, _cols(c)], AluOpType.add).then_inc(S.sy, 1)
+        for n, q in enumerate(order):
+            v.wait_ge(S["p%d" % q], NP)
+            if n == 0:
+                continue
+            if n > 1:
+                v.wait_ge(S.sadd, n - 1)
+            first = T.pl[:, _cols(order[0])] if n == 1 else T.acc[:, :]
+            if n < len(order) - 1:
+                v.tensor_tensor(T.acc[:, :], first, T.pl[:, _cols(q)], AluOpType.add).then_inc(S.sadd, 1)
+            else:
+                v.tensor_tensor(T.yout[:, :], first, T.pl[:, _cols(q)], AluOpType.add).then_inc(S.sy, 1)
         g.sync.wait_ge(S.sy, 1)
         g.sync.dma_start(T.y[:, :], T.yout[:, :]).then_inc(S.sst, 16)
         g.sync.wait_ge(S.sst, 16)
-        g.wait_ge(S.snd, 2 * NX + NE + NWON)
+        g.wait_ge(S.snd, sent)
         return
 
     for r, c in relay.items():
         if c == core:
-            k = where[r][1]
-            g.wait_ge(S.xown, NX)
-            g.remote_dma_fused([_tr(topo, T.xd[0], [T.xs[:, _cols(2)]], [site[groups[2][k]]], lo, S.xl0)],
-                               local_sem=S.snd)
+            gi, k = where[r]
+            xfwd(k, gi, 1, _xslots(gi)[2:3])
             g.wait_ge(S.snd, NE)
             return
 
-    owner = [r for r, c in site.items() if c == core]
-    if not owner:
+    kind = [t for t in range(2) for r, c in sites[t].items() if c == core]
+    if not kind:
         return
 
-    r = owner[0]
+    t = kind[0]
+    mine = sites[t]
+    r = [r for r, c in mine.items() if c == core][0]
     gi, k = where[r]
     slots = _xslots(gi)
     te, sc, ve = g.tensor, g.scalar, g.vector
 
-    g.wait_ge(S.xown, NX)
-    if gi == 0:
-        fwd = _tr(topo, T.xd[0], [T.xs[:, _cols(2)]], [site[groups[1][k]]], lo, S.xl0)
-    else:
-        fwd = _tr(topo, T.xd[0], [T.xs[:, _cols(gi)]], [site[groups[0][k]]], lo, S["xl%d" % (gi - 1)])
-    g.remote_dma_fused([fwd], local_sem=S.snd)
+    xfwd(k, gi, t, slots[1:2] if t == 1 else [gs for gs in slots[1:] if gi == 0 or gs == 0])
     sent = NE
+    if t == 1:
+        g.wait_ge(S["w%d" % k], NE)
+        half = T.wbuf[:, k * 256 + 128:(k + 1) * 256]
+        g.remote_dma_fused([_tr(topo, half, [half], [mine[groups[gi][(k + 2) % GS]]], lo, S["w%d" % k])],
+                           local_sem=S.snd)
+        sent += NE
 
     g.sync.wait_ge(S.xown, NX)
     g.sync.dma_start(T.xs[:, _cols(0)], T.xd[0]).then_inc(S.xe, 16)
-    early = 1
-    if gi != 0:
-        sc.wait_ge(S.xpeer, NX)
-        sc.dma_start(T.xs[:, _cols(1)], T.xd[1]).then_inc(S.xe, 16)
-        early = 2
+    late = []
+    for s in range(1, NJ):
+        if t == 0 and gi != 0 and slots[s] != 0:
+            g.sync.wait_ge(S.xpeer, NH)
+            g.sync.dma_start(T.xs[:, _cols(s)], T.xd[1]).then_inc(S.xe1, 16)
+            late.append((S.xe1, 16))
+        else:
+            late.append((S["xg%d" % slots[s]], NE))
 
-    jobs = [(0, early, [(S.xe, 16 * early)])]
-    for n, s in enumerate(range(early, NJ)):
-        jobs.append((s, 1, [(S["xl%d" % n], NE)]))
-    order = [(k - d) % GS for d in range(GS)]
+    H = TK // 2
+    own = [(S["w%d" % k], NE), (S.xe, 16)]
+    if t == 0:
+        m0, m1 = (k - 1) % GS, (k + 1) % GS
+        stages = [(k, 0, H, own, []), (m0, 0, NC, late + [(S["w%d" % m0], NE)], []),
+                  (m1, 0, NC, [(S["w%d" % m1], NE)], [])]
+        sets = [(0, H), (H, NC)]
+    else:
+        m0 = (k + 2) % GS
+        stages = [(k, H, TK, own, []), (k, TK, NC, late, []),
+                  (m0, 0, NC, [(S["v%d" % m0], NE)], [(S["w%d" % m0], NE)])]
+        sets = [(0, H), (H, TK), (TK, NC)]
+    uses = [[i for i, st in enumerate(stages) if st[1] <= a0 and a1 <= st[2]] for a0, a1 in sets]
 
-    for j, (s0, ns, waits) in enumerate(jobs):
-        c0, c1 = s0 * TK, (s0 + ns) * TK
+    def mm1(i):
+        m, c0, c1, waits, _ = stages[i]
         for sem, val in waits:
             te.wait_ge(sem, val)
+        te.matmul(T["hb%d" % i][:, c0:c1], T.wbuf[:, m * 256:m * 256 + 128], T.xs[:, c0:c1], True, True) \
+            .then_inc(S["m1_%d" % i], 1)
+        sc.wait_ge(S["m1_%d" % i], 1)
+        sc.activation(T.hs[:, i * NC + c0:i * NC + c1], T["hb%d" % i][:, c0:c1],
+                      ActivationFunctionType.Gelu_apprx_tanh).then_inc(S["ac_%d" % i], 1)
 
-        def mm1(i):
-            m = order[i]
-            if j == 0:
-                te.wait_ge(S["w%d" % m], NWON if m == k else NE)
-            hb = T["hb%d" % i]
-            te.matmul(hb[:, c0:c1], T.wbuf[:, m * 256:m * 256 + 128], T.xs[:, c0:c1], True, True) \
-                .then_inc(S["m1_%d_%d" % (j, i)], 1)
-            sc.wait_ge(S["m1_%d_%d" % (j, i)], 1)
-            sc.activation(T.hs[:, i * NJ * TK + c0:i * NJ * TK + c1], hb[:, c0:c1],
-                          ActivationFunctionType.Gelu_apprx_tanh).then_inc(S["ac_%d_%d" % (j, i)], 1)
+    def mm2(i):
+        m = stages[i][0]
+        for sem, val in stages[i][4]:
+            te.wait_ge(sem, val)
+        te.wait_ge(S["ac_%d" % i], 1)
+        n = 0
+        for b, (a0, a1) in enumerate(sets):
+            if i in uses[b]:
+                te.matmul(T["yb%d" % b][:, a0:a1], T.wbuf[:, m * 256 + 128:(m + 1) * 256],
+                          T.hs[:, i * NC + a0:i * NC + a1], i == uses[b][0], i == uses[b][-1]).then_inc(S.y2, 1)
+                n += 1
+        return n
 
-        def mm2(i):
-            m = order[i]
-            te.wait_ge(S["ac_%d_%d" % (j, i)], 1)
-            te.matmul(T["yb%d" % j][:, 0:c1 - c0], T.wbuf[:, m * 256 + 128:(m + 1) * 256],
-                      T.hs[:, i * NJ * TK + c0:i * NJ * TK + c1], i == 0, i == GS - 1) \
-                .then_inc(S["y2_%d" % j], 1)
+    done = 0
+    mm1(0)
+    for i in range(1, len(stages)):
+        mm1(i)
+        done += mm2(i - 1)
+    done += mm2(len(stages) - 1)
+    ve.wait_ge(S.y2, done)
+    for b, (a0, a1) in enumerate(sets):
+        ve.tensor_copy(T.ps[:, a0:a1], T["yb%d" % b][:, a0:a1]).then_inc(S.cp, 1)
 
-        mm1(0)
-        for i in range(1, GS):
-            mm1(i)
-            mm2(i - 1)
-        mm2(GS - 1)
-        ve.wait_ge(S["y2_%d" % j], GS)
-        ve.tensor_copy(T.ps[:, c0:c1], T["yb%d" % j][:, 0:c1 - c0]).then_inc(S["cp%d" % j], 1)
-
-        g.wait_ge(S["cp%d" % j], 1)
-        trs = []
-        for s in range(s0, s0 + ns):
-            dst = groups[slots[s]][k]
-            engs = hi if topo.chip(dst) == topo.chip(core) else lo
-            trs.append(_tr(topo, T.ps[:, _cols(s)], [T.pl[:, _cols(gi)]], [dst], engs[0:NE], S["p%d" % gi]))
-            sent += NE
-        g.remote_dma_fused(trs, local_sem=S.snd)
+    g.wait_ge(S.cp, len(sets))
+    q = 2 * gi + t
+    engs = [hi[0:NP], lo[0:NP], lo[NP:2 * NP]]
+    g.remote_dma_fused([_tr(topo, T.ps[:, _cols(s)], [T.pl[:, _cols(q)]], [groups[slots[s]][k]], engs[s],
+                            S["p%d" % q]) for s in range(NJ)], local_sem=S.snd)
+    sent += NJ * NP
     g.wait_ge(S.snd, sent)

@@ -11,7 +11,8 @@ SCRATCH = {
     "xsrc": ("dram", [128, TK], "bfloat16"),
     "wst": ("sbuf", [128, 256], "bfloat16"),
     "pl": ("sbuf", [128, 2 * NC], "bfloat16"),
-    "acc": ("sbuf", [128, TK], "float32"),
+    "ones": ("sbuf", [128, 128], "bfloat16"),
+    "ident": ("sbuf", [128, 128], "bfloat16"),
     "yout": ("sbuf", [128, TK], "bfloat16"),
     "xd": ("dram", [2, 128, TK], "bfloat16"),
     "xs": ("sbuf", [128, NC], "bfloat16"),
@@ -21,10 +22,12 @@ SCRATCH = {
 }
 for _i in range(NST):
     SCRATCH["hb%d" % _i] = ("psum", [128, 512], "float32")
+for _i in range(NJ):
     SCRATCH["yb%d" % _i] = ("psum", [128, 512], "float32")
 
-SEMAPHORES = ["ldx", "ldw", "snd", "sadd", "sy", "sst", "xown", "xpeer", "xe", "xe1", "y2", "cp"]
+SEMAPHORES = ["ldx", "ldw", "snd", "sadd", "sy", "sst", "xown", "xpeer", "xe", "xe1", "cp", "sone", "sid", "sz"]
 SEMAPHORES += ["xg%d" % _j for _j in range(NJ)] + ["p%d" % _j for _j in range(2 * NJ)]
+SEMAPHORES += ["yq%d" % _j for _j in range(NJ)]
 SEMAPHORES += ["w%d" % _i for _i in range(GS)] + ["v%d" % _i for _i in range(GS)]
 SEMAPHORES += ["m1_%d" % _i for _i in range(NST)] + ["ac_%d" % _i for _i in range(NST)]
 
@@ -39,14 +42,14 @@ def _plan(T, topo):
     g2 = [o for o in major if o not in g1]
     groups = [minor, g1, g2]
     every = range(topo.CHIPS * topo.CORES_PER_CHIP)
-    sites, relay = ({}, {}), {}
+    sites, relay, relay2 = ({}, {}), {}, {}
     for gi, grp in enumerate(groups):
         far = groups[1][0] if gi == 0 else groups[0][0]
         for r in grp:
             ports = [c for c in every if c != r and ch(c) == ch(r) and topo.may_write(c, far)]
-            sites[0][r] = [c for c in ports if topo.die(c) == topo.die(r)][0]
+            sites[0][r], relay2[r] = [c for c in ports if topo.die(c) == topo.die(r)][0:2]
             sites[1][r], relay[r] = [c for c in ports if topo.die(c) != topo.die(r)][0:2]
-    return groups, sites, relay
+    return groups, sites, relay, relay2
 
 
 def _engines(topo, core):
@@ -83,14 +86,13 @@ def _xslots(gi):
 
 
 def rank_program(g, core, T, topo):
-    groups, sites, relay = _plan(T, topo)
+    groups, sites, relay, relay2 = _plan(T, topo)
     A, B = sites
     S = T.sem
     lo, hi = _engines(topo, core)
     where = {r: (gi, k) for gi, grp in enumerate(groups) for k, r in enumerate(grp)}
     NE = len(lo)
-    NH = NE // 2
-    NP = NH
+    NP = NE // 2
     NX = 2
 
     def xfwd(k, gi, kind, to):
@@ -103,36 +105,41 @@ def rank_program(g, core, T, topo):
         g.sync.dma_start(T.xsrc[:, :], T.x[:, :]).then_inc(S.ldx, 16)
         g.scalar.dma_start(T.wst[:, 0:128], T.w1[:, :]).then_inc(S.ldw, 16)
         g.sync.dma_start(T.wst[:, 128:256], T.w2[:, :]).then_inc(S.ldw, 16)
+        g.vector.memset(T.ones[:, :], 1.0).then_inc(S.sone, 1)
         g.wait_ge(S.ldx, 16)
-        trs = [_tr(topo, T.xsrc[:, :], [T.xd[0], T.xd[0]], [B[core], relay[core]], hi[0:NX], S.xown),
-               _tr(topo, T.xsrc[:, :], [T.xd[0]], [A[core]], hi[NX:2 * NX], S.xown)]
-        sent = 2 * NX
-        if gi != 0:
-            trs.append(_tr(topo, T.xsrc[:, :], [T.xd[1]], [A[groups[3 - gi][k]]], lo[0:NH], S.xpeer))
-            sent += NH
+        trs = [_tr(topo, T.xsrc[:, :], [T.xd[0]], [B[core]], [hi[0], hi[2]], S.xown),
+               _tr(topo, T.xsrc[:, :], [T.xd[0]], [A[core]], [hi[1], hi[3]], S.xown),
+               _tr(topo, T.xsrc[:, :], [T.xd[0]], [relay[core]], [hi[4], hi[6]], S.xown)]
+        if gi == 0:
+            trs.append(_tr(topo, T.xsrc[:, :], [T.xd[0]], [relay2[core]], [hi[5], hi[7]], S.xown))
+        else:
+            trs.append(_tr(topo, T.xsrc[:, :], [T.xd[1]], [A[groups[3 - gi][k]]], [lo[0], lo[2]], S.xpeer))
+        sent = 4 * NX
         g.remote_dma_fused(trs, local_sem=S.snd)
         g.wait_ge(S.ldw, 32)
         slot = T.wbuf[:, k * 256:(k + 1) * 256]
-        nb = [A[groups[gi][(k + 1) % GS]], A[groups[gi][(k - 1) % GS]]]
+        s1, s2 = T.wbuf[:, k * 256:k * 256 + 128], T.wbuf[:, k * 256 + 128:(k + 1) * 256]
+        nxt, prv, opp = [groups[gi][(k + d) % GS] for d in (1, -1, 2)]
         g.remote_dma_fused([_tr(topo, T.wst[:, :], [slot, slot], [B[core], A[core]], hi, S["w%d" % k]),
-                            _tr(topo, T.wst[:, :], [slot, slot], nb, lo, S["w%d" % k])],
+                            _tr(topo, T.wst[:, :], [slot], [A[nxt]], lo, S["w%d" % k])], local_sem=S.snd)
+        g.remote_dma_fused([_tr(topo, T.wst[:, 0:128], [s1, s1], [B[opp], A[prv]], lo, S["v%d" % k])],
                            local_sem=S.snd)
-        g.remote_dma_fused([_tr(topo, T.wst[:, 0:128], [T.wbuf[:, k * 256:k * 256 + 128]],
-                                [B[groups[gi][(k + 2) % GS]]], lo, S["v%d" % k])], local_sem=S.snd)
-        sent += 3 * NE
+        g.remote_dma_fused([_tr(topo, T.wst[:, 128:256], [s2], [A[prv]], lo, S["w%d" % k])], local_sem=S.snd)
+        sent += 4 * NE
+        g.wait_ge(S.sone, 1)
+        g.affine_select(T.ident[:, :], T.ones[:, :], [[-1, 128]], AluOpType.is_equal, 0.0, 0, 1).then_inc(S.sid, 1)
         order = [2 * gs + t for gs in _xslots(gi) for t in range(2)]
-        v = g.vector
-        for n, q in enumerate(order):
-            v.wait_ge(S["p%d" % q], NP)
-            if n == 0:
-                continue
-            if n > 1:
-                v.wait_ge(S.sadd, n - 1)
-            first = T.pl[:, _cols(order[0])] if n == 1 else T.acc[:, :]
-            if n < len(order) - 1:
-                v.tensor_tensor(T.acc[:, :], first, T.pl[:, _cols(q)], AluOpType.add).then_inc(S.sadd, 1)
-            else:
-                v.tensor_tensor(T.yout[:, :], first, T.pl[:, _cols(q)], AluOpType.add).then_inc(S.sy, 1)
+        te, v = g.tensor, g.vector
+        te.wait_ge(S.sid, 1)
+        early = order[:-1]
+        for n, q in enumerate(early):
+            te.wait_ge(S["p%d" % q], NP)
+            mm = te.matmul(T.hb0[:, 0:TK], T.ident[:, :], T.pl[:, _cols(q)], n == 0, n == len(early) - 1)
+            if n == len(early) - 1:
+                mm.then_inc(S.sadd, 1)
+        v.wait_ge(S.sadd, 1)
+        v.wait_ge(S["p%d" % order[-1]], NP)
+        v.tensor_tensor(T.yout[:, :], T.hb0[:, 0:TK], T.pl[:, _cols(order[-1])], AluOpType.add).then_inc(S.sy, 1)
         g.sync.wait_ge(S.sy, 1)
         g.sync.dma_start(T.y[:, :], T.yout[:, :]).then_inc(S.sst, 16)
         g.sync.wait_ge(S.sst, 16)
@@ -146,6 +153,14 @@ def rank_program(g, core, T, topo):
             g.wait_ge(S.snd, NE)
             return
 
+    for r, c in relay2.items():
+        if c == core:
+            gi, k = where[r]
+            if gi == 0:
+                xfwd(k, gi, 0, _xslots(gi)[2:3])
+                g.wait_ge(S.snd, NE)
+            return
+
     kind = [t for t in range(2) for r, c in sites[t].items() if c == core]
     if not kind:
         return
@@ -156,8 +171,12 @@ def rank_program(g, core, T, topo):
     gi, k = where[r]
     slots = _xslots(gi)
     te, sc, ve = g.tensor, g.scalar, g.vector
+    H = TK // 2
 
-    xfwd(k, gi, t, slots[1:2] if t == 1 else [gs for gs in slots[1:] if gi == 0 or gs == 0])
+    z0 = H if t == 0 else 0
+    ve.memset(T.hs[:, z0:z0 + H], 0.0).then_inc(S.sz, 1)
+
+    xfwd(k, gi, t, slots[1:2] if (t == 1 or gi == 0) else [gs for gs in slots[1:] if gs == 0])
     sent = NE
     if t == 1:
         g.wait_ge(S["w%d" % k], NE)
@@ -171,60 +190,57 @@ def rank_program(g, core, T, topo):
     late = []
     for s in range(1, NJ):
         if t == 0 and gi != 0 and slots[s] != 0:
-            g.sync.wait_ge(S.xpeer, NH)
+            g.sync.wait_ge(S.xpeer, NX)
             g.sync.dma_start(T.xs[:, _cols(s)], T.xd[1]).then_inc(S.xe1, 16)
             late.append((S.xe1, 16))
         else:
             late.append((S["xg%d" % slots[s]], NE))
 
-    H = TK // 2
     own = [(S["w%d" % k], NE), (S.xe, 16)]
     if t == 0:
         m0, m1 = (k - 1) % GS, (k + 1) % GS
-        stages = [(k, 0, H, own, []), (m0, 0, NC, late + [(S["w%d" % m0], NE)], []),
-                  (m1, 0, NC, [(S["w%d" % m1], NE)], [])]
-        sets = [(0, H), (H, NC)]
+        first = [(k, 0, H, 0, own), (m0, 0, NC, 1, late + [(S["w%d" % m0], NE)]), (m1, 0, NC, 2, [(S["v%d" % m1], NE)])]
+        second = [(k, 0, [(S.ac_0, 1), (S.sz, 1)], [0], [True], False),
+                  (m0, 1, [(S.ac_1, 1)], [0, 1, 2], [False, True, True], False),
+                  (m1, 2, [(S["w%d" % m1], NE), (S.ac_2, 1)], [0, 1, 2], [False, False, False], True)]
+        prog = [(1, 0), (1, 1), (2, 0), (1, 2), (2, 1), (2, 2)]
     else:
         m0 = (k + 2) % GS
-        stages = [(k, H, TK, own, []), (k, TK, NC, late, []),
-                  (m0, 0, NC, [(S["v%d" % m0], NE)], [(S["w%d" % m0], NE)])]
-        sets = [(0, H), (H, TK), (TK, NC)]
-    uses = [[i for i, st in enumerate(stages) if st[1] <= a0 and a1 <= st[2]] for a0, a1 in sets]
+        first = [(k, H, TK, 0, own), (k, TK, NC, 0, late), (m0, 0, NC, 2, [(S["v%d" % m0], NE)])]
+        second = [(k, 0, [(S.ac_0, 1), (S.ac_1, 1), (S.sz, 1)], [0, 1, 2], [True, True, True], False),
+                  (m0, 2, [(S["w%d" % m0], NE), (S.ac_2, 1)], [0, 1, 2], [False, False, False], True)]
+        prog = [(1, 0), (1, 1), (1, 2), (2, 0), (2, 1)]
 
-    def mm1(i):
-        m, c0, c1, waits, _ = stages[i]
-        for sem, val in waits:
-            te.wait_ge(sem, val)
-        te.matmul(T["hb%d" % i][:, c0:c1], T.wbuf[:, m * 256:m * 256 + 128], T.xs[:, c0:c1], True, True) \
-            .then_inc(S["m1_%d" % i], 1)
-        sc.wait_ge(S["m1_%d" % i], 1)
-        sc.activation(T.hs[:, i * NC + c0:i * NC + c1], T["hb%d" % i][:, c0:c1],
-                      ActivationFunctionType.Gelu_apprx_tanh).then_inc(S["ac_%d" % i], 1)
+    cnt = [0] * NJ
+    for what, i in prog:
+        if what == 1:
+            m, c0, c1, hsl, waits = first[i]
+            for sem, val in waits:
+                te.wait_ge(sem, val)
+            te.matmul(T["hb%d" % i][:, c0:c1], T.wbuf[:, m * 256:m * 256 + 128], T.xs[:, c0:c1], True, True) \
+                .then_inc(S["m1_%d" % i], 1)
+            sc.wait_ge(S["m1_%d" % i], 1)
+            sc.activation(T.hs[:, hsl * NC + c0:hsl * NC + c1], T["hb%d" % i][:, c0:c1],
+                          ActivationFunctionType.Gelu_apprx_tanh).then_inc(S["ac_%d" % i], 1)
+        else:
+            m, hsl, waits, blocks, starts, stop = second[i]
+            for sem, val in waits:
+                te.wait_ge(sem, val)
+            for j, st in zip(blocks, starts):
+                te.matmul(T["yb%d" % j][:, _cols(j)], T.wbuf[:, m * 256 + 128:(m + 1) * 256],
+                          T.hs[:, hsl * NC + j * TK:hsl * NC + (j + 1) * TK], st, stop).then_inc(S["yq%d" % j], 1)
+                cnt[j] += 1
 
-    def mm2(i):
-        m = stages[i][0]
-        for sem, val in stages[i][4]:
-            te.wait_ge(sem, val)
-        te.wait_ge(S["ac_%d" % i], 1)
-        n = 0
-        for b, (a0, a1) in enumerate(sets):
-            if i in uses[b]:
-                te.matmul(T["yb%d" % b][:, a0:a1], T.wbuf[:, m * 256 + 128:(m + 1) * 256],
-                          T.hs[:, i * NC + a0:i * NC + a1], i == uses[b][0], i == uses[b][-1]).then_inc(S.y2, 1)
-                n += 1
-        return n
+    for j in range(NJ):
+        if j % 2 == 0:
+            ve.wait_ge(S["yq%d" % j], cnt[j])
+            ve.tensor_copy(T.ps[:, _cols(j)], T["yb%d" % j][:, _cols(j)]).then_inc(S.cp, 1)
+        else:
+            sc.wait_ge(S["yq%d" % j], cnt[j])
+            sc.activation(T.ps[:, _cols(j)], T["yb%d" % j][:, _cols(j)], ActivationFunctionType.Copy) \
+                .then_inc(S.cp, 1)
 
-    done = 0
-    mm1(0)
-    for i in range(1, len(stages)):
-        mm1(i)
-        done += mm2(i - 1)
-    done += mm2(len(stages) - 1)
-    ve.wait_ge(S.y2, done)
-    for b, (a0, a1) in enumerate(sets):
-        ve.tensor_copy(T.ps[:, a0:a1], T["yb%d" % b][:, a0:a1]).then_inc(S.cp, 1)
-
-    g.wait_ge(S.cp, len(sets))
+    g.wait_ge(S.cp, NJ)
     q = 2 * gi + t
     engs = [hi[0:NP], lo[0:NP], lo[NP:2 * NP]]
     g.remote_dma_fused([_tr(topo, T.ps[:, _cols(s)], [T.pl[:, _cols(q)]], [groups[slots[s]][k]], engs[s],

from concourse.bass import DstId, RemoteDMATransfer
from concourse.mybir import AluOpType, ActivationFunctionType

TK = 64
GS = 4
NJ = 3
NC = NJ * TK
NST = 3

SCRATCH = {
    "xsrc": ("dram", [128, TK], "bfloat16"),
    "wst": ("sbuf", [128, 256], "bfloat16"),
    "pl": ("sbuf", [128, 2 * NC], "bfloat16"),
    "ones": ("sbuf", [128, 128], "bfloat16"),
    "ident": ("sbuf", [128, 128], "bfloat16"),
    "yout": ("sbuf", [128, TK], "bfloat16"),
    "xd": ("dram", [2, 128, TK], "bfloat16"),
    "xs": ("sbuf", [128, NC], "bfloat16"),
    "wbuf": ("sbuf", [128, GS * 256], "bfloat16"),
    "hs": ("sbuf", [128, NST * NC], "bfloat16"),
    "ps": ("sbuf", [128, NC], "bfloat16"),
}
for _i in range(NST):
    SCRATCH["hb%d" % _i] = ("psum", [128, 512], "float32")
for _i in range(NJ):
    SCRATCH["yb%d" % _i] = ("psum", [128, 512], "float32")

SEMAPHORES = ["ldx", "ldw", "snd", "sadd", "sy", "sst", "xown", "xpeer", "xe", "xe1", "cp", "sone", "sid", "sz"]
SEMAPHORES += ["xg%d" % _j for _j in range(NJ)] + ["p%d" % _j for _j in range(2 * NJ)]
SEMAPHORES += ["yq%d" % _j for _j in range(NJ)]
SEMAPHORES += ["w%d" % _i for _i in range(GS)] + ["v%d" % _i for _i in range(GS)]
SEMAPHORES += ["m1_%d" % _i for _i in range(NST)] + ["ac_%d" % _i for _i in range(NST)]


def _plan(T, topo):
    ch = topo.chip
    ranks = list(T.cores)
    a = [r for r in ranks if ch(r) == ch(ranks[0]) or topo.same_plane(ch(r), ch(ranks[0]))]
    b = [r for r in ranks if r not in a]
    minor, major = (a, b) if len(a) < len(b) else (b, a)
    g1 = [o for e in minor for o in major if topo.mates(ch(e), ch(o))]
    g2 = [o for o in major if o not in g1]
    groups = [minor, g1, g2]
    every = range(topo.CHIPS * topo.CORES_PER_CHIP)
    sites, relay, relay2 = ({}, {}), {}, {}
    for gi, grp in enumerate(groups):
        far = groups[1][0] if gi == 0 else groups[0][0]
        for r in grp:
            ports = [c for c in every if c != r and ch(c) == ch(r) and topo.may_write(c, far)]
            sites[0][r], relay2[r] = [c for c in ports if topo.die(c) == topo.die(r)][0:2]
            sites[1][r], relay[r] = [c for c in ports if topo.die(c) != topo.die(r)][0:2]
    return groups, sites, relay, relay2


def _engines(topo, core):
    every = range(topo.CHIPS * topo.CORES_PER_CHIP)
    near = [c for c in every if c != core and topo.chip(c) == topo.chip(core)][0]
    far = [c for c in every if topo.chip(c) != topo.chip(core)][0]
    on, off = topo.mask(core, near), topo.mask(core, far)
    lo = [e for e in range(on.bit_length()) if (off >> e) & 1]
    hi = [e for e in range(on.bit_length()) if (on >> e) & 1 and not (off >> e) & 1]
    return lo, hi


def _mask(engs):
    m = 0
    for e in engs:
        m |= 1 << e
    return m


def _tr(topo, src, dsts, cores, engs, sem):
    ids = []
    for c in cores:
        rid, pid, _ = topo.addr(c)
        ids.append(DstId(rid=rid, pnc=pid))
    return RemoteDMATransfer(dst_ids=ids, dma_engine_mask=_mask(engs), remote_sem=sem, srcs=[src], dsts=list(dsts))


def _cols(j):
    return slice(j * TK, (j + 1) * TK)


def _xslots(gi):
    return [[0, 1, 2], [1, 2, 0], [2, 1, 0]][gi]


def rank_program(g, core, T, topo):
    groups, sites, relay, relay2 = _plan(T, topo)
    A, B = sites
    S = T.sem
    lo, hi = _engines(topo, core)
    where = {r: (gi, k) for gi, grp in enumerate(groups) for k, r in enumerate(grp)}
    NE = len(lo)
    NP = NE // 2
    NX = 2

    def xfwd(k, gi, kind, to):
        g.wait_ge(S.xown, NX)
        g.remote_dma_fused([_tr(topo, T.xd[0], [T.xs[:, _cols(_xslots(gs).index(gi))] for gs in to],
                                [sites[kind][groups[gs][k]] for gs in to], lo, S["xg%d" % gi])], local_sem=S.snd)

    if core in where:
        gi, k = where[core]
        g.sync.dma_start(T.xsrc[:, :], T.x[:, :]).then_inc(S.ldx, 16)
        g.scalar.dma_start(T.wst[:, 0:128], T.w1[:, :]).then_inc(S.ldw, 16)
        g.sync.dma_start(T.wst[:, 128:256], T.w2[:, :]).then_inc(S.ldw, 16)
        g.vector.memset(T.ones[:, :], 1.0).then_inc(S.sone, 1)
        g.wait_ge(S.ldx, 16)
        trs = [_tr(topo, T.xsrc[:, :], [T.xd[0]], [B[core]], [hi[0], hi[2]], S.xown),
               _tr(topo, T.xsrc[:, :], [T.xd[0]], [A[core]], [hi[1], hi[3]], S.xown),
               _tr(topo, T.xsrc[:, :], [T.xd[0]], [relay[core]], [hi[4], hi[6]], S.xown)]
        if gi == 0:
            trs.append(_tr(topo, T.xsrc[:, :], [T.xd[0]], [relay2[core]], [hi[5], hi[7]], S.xown))
        else:
            trs.append(_tr(topo, T.xsrc[:, :], [T.xd[1]], [A[groups[3 - gi][k]]], [lo[0], lo[2]], S.xpeer))
        sent = 4 * NX
        g.remote_dma_fused(trs, local_sem=S.snd)
        g.wait_ge(S.ldw, 32)
        slot = T.wbuf[:, k * 256:(k + 1) * 256]
        s1, s2 = T.wbuf[:, k * 256:k * 256 + 128], T.wbuf[:, k * 256 + 128:(k + 1) * 256]
        nxt, prv, opp = [groups[gi][(k + d) % GS] for d in (1, -1, 2)]
        g.remote_dma_fused([_tr(topo, T.wst[:, :], [slot, slot], [B[core], A[core]], hi, S["w%d" % k]),
                            _tr(topo, T.wst[:, :], [slot], [A[nxt]], lo, S["w%d" % k])], local_sem=S.snd)
        g.remote_dma_fused([_tr(topo, T.wst[:, 0:128], [s1, s1], [B[opp], A[prv]], lo, S["v%d" % k])],
                           local_sem=S.snd)
        g.remote_dma_fused([_tr(topo, T.wst[:, 128:256], [s2], [A[prv]], lo, S["w%d" % k])], local_sem=S.snd)
        sent += 4 * NE
        g.wait_ge(S.sone, 1)
        g.affine_select(T.ident[:, :], T.ones[:, :], [[-1, 128]], AluOpType.is_equal, 0.0, 0, 1).then_inc(S.sid, 1)
        order = [2 * gs + t for gs in _xslots(gi) for t in range(2)]
        te, v = g.tensor, g.vector
        te.wait_ge(S.sid, 1)
        early = order[:-1]
        for n, q in enumerate(early):
            te.wait_ge(S["p%d" % q], NP)
            mm = te.matmul(T.hb0[:, 0:TK], T.ident[:, :], T.pl[:, _cols(q)], n == 0, n == len(early) - 1)
            if n == len(early) - 1:
                mm.then_inc(S.sadd, 1)
        v.wait_ge(S.sadd, 1)
        v.wait_ge(S["p%d" % order[-1]], NP)
        v.tensor_tensor(T.yout[:, :], T.hb0[:, 0:TK], T.pl[:, _cols(order[-1])], AluOpType.add).then_inc(S.sy, 1)
        g.sync.wait_ge(S.sy, 1)
        g.sync.dma_start(T.y[:, :], T.yout[:, :]).then_inc(S.sst, 16)
        g.sync.wait_ge(S.sst, 16)
        g.wait_ge(S.snd, sent)
        return

    for r, c in relay.items():
        if c == core:
            gi, k = where[r]
            xfwd(k, gi, 1, _xslots(gi)[2:3])
            g.wait_ge(S.snd, NE)
            return

    for r, c in relay2.items():
        if c == core:
            gi, k = where[r]
            if gi == 0:
                xfwd(k, gi, 0, _xslots(gi)[2:3])
                g.wait_ge(S.snd, NE)
            return

    kind = [t for t in range(2) for r, c in sites[t].items() if c == core]
    if not kind:
        return

    t = kind[0]
    mine = sites[t]
    r = [r for r, c in mine.items() if c == core][0]
    gi, k = where[r]
    slots = _xslots(gi)
    te, sc, ve = g.tensor, g.scalar, g.vector
    H = TK // 2

    z0 = H if t == 0 else 0
    ve.memset(T.hs[:, z0:z0 + H], 0.0).then_inc(S.sz, 1)

    xfwd(k, gi, t, slots[1:2] if (t == 1 or gi == 0) else [gs for gs in slots[1:] if gs == 0])
    sent = NE
    if t == 1:
        g.wait_ge(S["w%d" % k], NE)
        half = T.wbuf[:, k * 256 + 128:(k + 1) * 256]
        g.remote_dma_fused([_tr(topo, half, [half], [mine[groups[gi][(k + 2) % GS]]], lo, S["w%d" % k])],
                           local_sem=S.snd)
        sent += NE

    g.sync.wait_ge(S.xown, NX)
    g.sync.dma_start(T.xs[:, _cols(0)], T.xd[0]).then_inc(S.xe, 16)
    late = []
    for s in range(1, NJ):
        if t == 0 and gi != 0 and slots[s] != 0:
            g.sync.wait_ge(S.xpeer, NX)
            g.sync.dma_start(T.xs[:, _cols(s)], T.xd[1]).then_inc(S.xe1, 16)
            late.append((S.xe1, 16))
        else:
            late.append((S["xg%d" % slots[s]], NE))

    own = [(S["w%d" % k], NE), (S.xe, 16)]
    if t == 0:
        m0, m1 = (k - 1) % GS, (k + 1) % GS
        first = [(k, 0, H, 0, own), (m0, 0, NC, 1, late + [(S["w%d" % m0], NE)]), (m1, 0, NC, 2, [(S["v%d" % m1], NE)])]
        second = [(k, 0, [(S.ac_0, 1), (S.sz, 1)], [0], [True], False),
                  (m0, 1, [(S.ac_1, 1)], [0, 1, 2], [False, True, True], False),
                  (m1, 2, [(S["w%d" % m1], NE), (S.ac_2, 1)], [0, 1, 2], [False, False, False], True)]
        prog = [(1, 0), (1, 1), (2, 0), (1, 2), (2, 1), (2, 2)]
    else:
        m0 = (k + 2) % GS
        first = [(k, H, TK, 0, own), (k, TK, NC, 0, late), (m0, 0, NC, 2, [(S["v%d" % m0], NE)])]
        second = [(k, 0, [(S.ac_0, 1), (S.ac_1, 1), (S.sz, 1)], [0, 1, 2], [True, True, True], False),
                  (m0, 2, [(S["w%d" % m0], NE), (S.ac_2, 1)], [0, 1, 2], [False, False, False], True)]
        prog = [(1, 0), (1, 1), (1, 2), (2, 0), (2, 1)]

    cnt = [0] * NJ
    for what, i in prog:
        if what == 1:
            m, c0, c1, hsl, waits = first[i]
            for sem, val in waits:
                te.wait_ge(sem, val)
            te.matmul(T["hb%d" % i][:, c0:c1], T.wbuf[:, m * 256:m * 256 + 128], T.xs[:, c0:c1], True, True) \
                .then_inc(S["m1_%d" % i], 1)
            sc.wait_ge(S["m1_%d" % i], 1)
            sc.activation(T.hs[:, hsl * NC + c0:hsl * NC + c1], T["hb%d" % i][:, c0:c1],
                          ActivationFunctionType.Gelu_apprx_tanh).then_inc(S["ac_%d" % i], 1)
        else:
            m, hsl, waits, blocks, starts, stop = second[i]
            for sem, val in waits:
                te.wait_ge(sem, val)
            for j, st in zip(blocks, starts):
                te.matmul(T["yb%d" % j][:, _cols(j)], T.wbuf[:, m * 256 + 128:(m + 1) * 256],
                          T.hs[:, hsl * NC + j * TK:hsl * NC + (j + 1) * TK], st, stop).then_inc(S["yq%d" % j], 1)
                cnt[j] += 1

    for j in range(NJ):
        if j % 2 == 0:
            ve.wait_ge(S["yq%d" % j], cnt[j])
            ve.tensor_copy(T.ps[:, _cols(j)], T["yb%d" % j][:, _cols(j)]).then_inc(S.cp, 1)
        else:
            sc.wait_ge(S["yq%d" % j], cnt[j])
            sc.activation(T.ps[:, _cols(j)], T["yb%d" % j][:, _cols(j)], ActivationFunctionType.Copy) \
                .then_inc(S.cp, 1)

    g.wait_ge(S.cp, NJ)
    q = 2 * gi + t
    engs = [hi[0:NP], lo[0:NP], lo[NP:2 * NP]]
    g.remote_dma_fused([_tr(topo, T.ps[:, _cols(s)], [T.pl[:, _cols(q)]], [groups[slots[s]][k]], engs[s],
                            S["p%d" % q]) for s in range(NJ)], local_sem=S.snd)
    sent += NJ * NP
    g.wait_ge(S.snd, sent)
